import numpy as np
import ml_dtypes


def mxq(x, axis, fmt="e4m3"):
    dtype, down = {"e4m3": (ml_dtypes.float8_e4m3fn, 7), "e5m2": (ml_dtypes.float8_e5m2, 14)}[fmt]
    v = np.moveaxis(np.asarray(x, np.float32).astype(ml_dtypes.bfloat16).astype(np.float64), axis, -1)
    blocks = v.reshape(v.shape[:-1] + (-1, 32))
    amax = np.abs(blocks).max(-1, keepdims=True)
    byte = np.maximum(np.where(amax > 0, np.frexp(amax)[1] - 1 + 127, 0) - down, 1)
    scale = np.exp2(byte - 127.0)
    codes = (blocks / scale).astype(np.float32).astype(dtype).astype(np.float64)
    return np.moveaxis((codes * scale).reshape(v.shape), -1, axis)


WIDE = False


def mx_kscale(k):
    if not WIDE:
        return np.ones(k)
    levels = np.array([10, -10, 5, -5, 0])
    if k % 512:
        return np.exp2(np.random.permutation(np.resize(levels, k // 32))).repeat(32)
    a = np.empty((k // 512, 16))
    for p in range(k // 512):
        a[p, :8] = np.random.permutation(np.resize(levels, 8))
        for g in range(8):
            far = levels[np.abs(levels - a[p, g]) >= 10]
            a[p, g + 8] = far[np.random.randint(len(far))]
    return np.exp2(a.ravel()).repeat(32)


BF16 = ml_dtypes.bfloat16


def bf(x):
    return np.asarray(x, np.float32).astype(BF16)


def f64(x):
    return np.asarray(x).astype(np.float64)

def planes(Y):
    n, m = Y.shape
    b = f64(bf(Y)).reshape(n // 32, 32, m)
    amax = np.abs(b).max(1)
    byte = np.clip(np.where(amax > 0, np.frexp(amax)[1] - 1 + 127 - 7, 1), 1, 254)
    codes = (b * np.exp2(127.0 - byte)[:, None, :]).reshape(n, m).astype(np.float32).astype(ml_dtypes.float8_e4m3fn).view(np.uint8)
    words = codes.reshape(n // 512, 128, 4, m).transpose(0, 1, 3, 2)
    return np.ascontiguousarray(words), np.ascontiguousarray(byte.astype(np.uint8).reshape(n // 512, 16, m))


F, N = 1024, 1024


def sigmoid(v):
    return 1.0 / (1.0 + np.exp(-v))


def focusing_window(td, t):
    td_col = td[:, None]
    t_row = t[None, :]
    return sigmoid(4.0 * (td_col + t_row)) * sigmoid(4.0 * (td_col - t_row))


def setup_inputs():
    s, g = mx_kscale(N), mx_kscale(N)
    a = 1.0 / np.sqrt(N)
    return {"f": bf(np.random.standard_normal((F, N)) * s),
            "r": bf(np.random.standard_normal((N, N)) * a / s[:, None] * g),
            "c": bf(np.random.standard_normal((N, N)) * a / g[:, None]),
            "fd": bf(np.random.standard_normal((F, N)) * 0.5),
            "td": bf(np.random.uniform(0.5, 2.0, F)),
            "t": bf(np.random.standard_normal(N))}


def core(f, r, c, fd, td, t):
    theta = focusing_window(f64(td), f64(t))
    u = mxq(f64(f), 1, "e4m3") @ mxq(f64(r), 0, "e4m3")
    fm = theta * u
    k = mxq(fm, 1, "e4m3") @ mxq(f64(c), 0, "e4m3")
    return f64(fd) + theta * k


def reference(f, r, c, fd, td, t):
    R_out = core(f, r, c, fd, td, t)
    words, scales = planes(R_out.T)
    return R_out, words, scales

@@ -1,0 +1,498 @@
+from contextlib import ExitStack
+
+import concourse.mybir as mybir
+from concourse.masks import make_identity
+
+F32 = mybir.dt.float32
+BF16 = mybir.dt.bfloat16
+I32 = mybir.dt.int32
+U32 = mybir.dt.uint32
+U8 = mybir.dt.uint8
+FP8X4 = mybir.dt.float8_e4m3fn_x4
+ACT = mybir.ActivationFunctionType
+ALU = mybir.AluOpType
+
+P = 128
+N = 1024
+TILES = 8
+HALF = 512
+WORD_GROUPS = ((0, 2), (2, 4), (4, 7), (7, 8))
+SCALE_GROUPS = ((0, 5), (5, 8))
+FLOPS = 2 * 2 * N * N * N
+
+
+def tile_marchenkofocusingiteration_x1_kernel(tc, f, r, c, fd, td, t, out_0, out_1, out_2):
+    nc = tc.nc
+    with ExitStack() as ctx:
+        keep = ctx.enter_context(tc.tile_pool(name="keep", bufs=1))
+        work = ctx.enter_context(tc.tile_pool(name="work", bufs=3))
+        psum = ctx.enter_context(tc.psum_pool(name="psum", bufs=2))
+        ctx.enter_context(tc.manual_schedule())
+
+        ident = keep.tile([P, P], F32, name="ident")
+        times = keep.tile([P, P + 16], BF16, name="times")
+        warm = keep.tile([P, 8], F32, name="warm")
+        raw = {}
+        grouped = {}
+        codes = {}
+        scales = {}
+        f_rows = {}
+        fd_rows = {}
+        sig = {}
+        acc = {}
+        fm = {}
+        turned = {}
+        res = {}
+        res16 = {}
+        words = {}
+        out_scales = {}
+        weights = {"r": r, "c": c}
+
+        def load_w(w, g, h):
+            raw[w, g, h] = keep.tile([P, 4, HALF], BF16, name="raw_%s%d%d" % (w, g, h))
+            rows = weights[w][512 * g : 512 * (g + 1), HALF * h : HALF * (h + 1)]
+            nc.sync.dma_start(out=raw[w, g, h][:], in_=rows.rearrange("(p j) n -> p j n", j=4))
+
+        def load_f(i):
+            f_rows[i] = keep.tile([P, N], BF16, name="f_rows%d" % i)
+            nc.sync.dma_start(out=f_rows[i][:], in_=f[P * i : P * (i + 1), :])
+
+        def load_fd(i):
+            fd_rows[i] = keep.tile([P, N], BF16, name="fd_rows%d" % i)
+            nc.sync.dma_start(out=fd_rows[i][:], in_=fd[P * i : P * (i + 1), :])
+
+        def interleave(eng, w, g, h, lo, hi):
+            if (w, g, h) not in grouped:
+                grouped[w, g, h] = work.tile([P, HALF, 4], BF16, name="grouped_%s%d%d" % (w, g, h), tag="wgrouped", bufs=4, align_bytes=64)
+            dst = grouped[w, g, h][:, lo:hi, :].rearrange("p (n i) j -> p n j i", i=4)
+            src = raw[w, g, h][:, :, lo:hi].rearrange("p j (n i) -> p n j i", i=4)
+            if eng == "v":
+                nc.vector.tensor_copy(out=dst, in_=src)
+            else:
+                nc.scalar.copy(out=dst, in_=src)
+
+        def quant_w(w, g, h):
+            codes[w, g, h] = keep.tile([P, HALF], U32, name="codes_%s%d%d" % (w, g, h), align_bytes=64)
+            scales[w, g, h] = keep.tile([P, HALF], U8, name="scales_%s%d%d" % (w, g, h), align_bytes=64)
+            nc.vector.quantize_mx(out=codes[w, g, h][:].bitcast(FP8X4), scales=scales[w, g, h][:], in_=grouped[w, g, h][:].rearrange("p n j -> p (n j)"))
+
+        def turn(kind, i):
+            src = {"f": f_rows, "fm": fm, "out": res16}[kind][i][:].bitcast(F32)
+            bank = psum.tile([P, 2, 2, P], F32, name="turned_%s%d" % (kind, i), tag="turned", bufs=4)
+            turned[kind, i] = bank
+            for g in range(2):
+                for u in range(2):
+                    if kind == "out":
+                        cols = src[:, 256 * g + P * u : 256 * g + P * (u + 1)]
+                    else:
+                        cols = src[:, 256 * g + u : 256 * (g + 1) : 2]
+                    nc.tensor.transpose(bank[:, g, u, :], cols, ident[:])
+
+        def copy(eng, out, in_):
+            if eng == "v":
+                nc.vector.tensor_copy(out=out, in_=in_)
+            else:
+                nc.scalar.copy(out=out, in_=in_)
+
+        def gather(eng, kind, i):
+            grouped[kind, i] = work.tile([P, 2, P, 4], BF16, name="grouped_%s%d" % (kind, i), tag="grouped_" + kind, bufs=8 if kind == "out" else 3, align_bytes=64)
+            dst = grouped[kind, i][:].rearrange("p g m j -> p (g m j)").bitcast(F32).rearrange("p (g m u) -> p g m u", g=2, u=2)
+            copy(eng, dst, turned[kind, i][:].rearrange("p g u m -> p g m u"))
+
+        def quant(kind, i):
+            codes[kind, i] = work.tile([P, 2 * P], U32, name="codes_%s%d" % (kind, i), tag="codes_" + kind, bufs=4, align_bytes=64)
+            scales[kind, i] = work.tile([P, 2 * P], U8, name="scales_%s%d" % (kind, i), tag="scales_" + kind, bufs=4, align_bytes=64)
+            nc.vector.quantize_mx(out=codes[kind, i][:].bitcast(FP8X4), scales=scales[kind, i][:], in_=grouped[kind, i][:].rearrange("p g m j -> p (g m j)"))
+
+        def multiply(kind, i, h):
+            w = {"f": "r", "fm": "c"}[kind]
+            acc[kind, i, h] = psum.tile([P, HALF], F32, name="acc_%s%d%d" % (kind, i, h), tag="acc_" + kind)
+            for g in range(2):
+                nc.tensor.matmul_mx(
+                    out=acc[kind, i, h][:],
+                    lhsT=codes[kind, i][:, P * g : P * (g + 1)].bitcast(FP8X4),
+                    lhsT_scale=scales[kind, i][:, P * g : P * (g + 1)],
+                    rhs=codes[w, g, h][:].bitcast(FP8X4),
+                    rhs_scale=scales[w, g, h][:],
+                    start=(g == 0),
+                    stop=(g == 1),
+                )
+
+        def window(i):
+            sig[i] = work.tile([P, N], F32, name="sig%d" % i, tag="sig", bufs=6)
+            nc.scalar.activation(out=sig[i][:], in_=log_t[:], func=ACT.Sigmoid, scale=-1.0, bias=log_td[:, i : i + 1])
+
+        def windowed(kind, i, h):
+            cols = slice(HALF * h, HALF * (h + 1))
+            if kind == "f":
+                if h == 0:
+                    fm[i] = work.tile([P, N], BF16, name="fm%d" % i, tag="fm")
+                dst = fm[i]
+            else:
+                if h == 0:
+                    res[i] = work.tile([P, N], F32, name="res%d" % i, tag="res", bufs=8)
+                dst = res[i]
+            nc.vector.scalar_tensor_tensor(out=dst[:, cols], in0=acc[kind, i, h][:], scalar=peak[:, i : i + 1], in1=sig[i][:, cols], op0=ALU.mult, op1=ALU.mult)
+
+        def add_direct(eng, i, h):
+            cols = slice(HALF * h, HALF * (h + 1))
+            eng.tensor_tensor(out=res[i][:, cols], in0=res[i][:, cols], in1=fd_rows[i][:, cols], op=ALU.add)
+
+        def store_res(i, lo, hi):
+            nc.sync.dma_start(out=out_0[P * i : P * (i + 1), lo:hi], in_=res[i][:, lo:hi])
+
+        def cast(eng, i, h):
+            cols = slice(HALF * h, HALF * (h + 1))
+            if h == 0:
+                res16[i] = work.tile([P, N], BF16, name="res16_%d" % i, tag="res16", bufs=4)
+            copy(
+                eng,
+                res16[i][:, cols].rearrange("p (u q e) -> p u q e", u=2, e=2),
+                res[i][:, cols].rearrange("p (q u e) -> p u q e", u=2, e=2),
+            )
+
+        def group_of(groups, i):
+            return [span for span in groups if span[0] <= i < span[1]][0]
+
+        def quant_out(i, g):
+            lo, hi = group_of(WORD_GROUPS, i)
+            if (lo, hi) not in words:
+                words[lo, hi] = keep.tile([P, 2, P * (hi - lo)], U32, name="words%d" % lo, align_bytes=64)
+            s_lo, s_hi = group_of(SCALE_GROUPS, i)
+            if (s_lo, s_hi) not in out_scales:
+                out_scales[s_lo, s_hi] = keep.tile([P, 2, P * (s_hi - s_lo)], U8, name="out_scales%d" % s_lo, align_bytes=64)
+            nc.vector.quantize_mx(
+                out=words[lo, hi][:, g, P * (i - lo) : P * (i - lo + 1)].bitcast(FP8X4),
+                scales=out_scales[s_lo, s_hi][:, g, P * (i - s_lo) : P * (i - s_lo + 1)],
+                in_=grouped["out", i][:, g, :, :].rearrange("p m j -> p (m j)"),
+            )
+
+        def store_words(k):
+            lo, hi = WORD_GROUPS[k]
+            dst = out_1.rearrange("g p m t -> p g (m t)").bitcast(I32)
+            nc.sync.dma_start(out=dst[:, :, P * lo : P * hi], in_=words[lo, hi][:].bitcast(I32))
+
+        def store_scales(k):
+            s_lo, s_hi = SCALE_GROUPS[k]
+            for q in range(4):
+                queue = nc.scalar if (s_hi == TILES and q < 2) else nc.sync
+                queue.dma_start(
+                    out=out_2[:, 4 * q : 4 * q + 4, P * s_lo : P * s_hi].rearrange("g r m -> r g m").bitcast(I32),
+                    in_=out_scales[s_lo, s_hi][32 * q : 32 * q + 4, :, :].bitcast(I32),
+                )
+
+        def add_rounded(i, h):
+            cols = slice(HALF * h, HALF * (h + 1))
+            nc.vector.tensor_tensor(
+                out=res16[i][:, cols].rearrange("p (u q e) -> p u q e", u=2, e=2),
+                in0=res[i][:, cols].rearrange("p (q u e) -> p u q e", u=2, e=2),
+                in1=fd_rows[i][:, cols].rearrange("p (q u e) -> p u q e", u=2, e=2),
+                op=ALU.add,
+            )
+
+        def turn_half(i, g):
+            src = res16[i][:].bitcast(F32)
+            turned["out", i, g] = psum.tile([P, 2, P], F32, name="turned_out%d%d" % (i, g), tag="turned", bufs=4)
+            for u in range(2):
+                nc.tensor.transpose(turned["out", i, g][:, u, :], src[:, 256 * g + P * u : 256 * g + P * (u + 1)], ident[:])
+
+        def gather_half(eng, i, g):
+            if g == 0:
+                grouped["out", i] = work.tile([P, 2, P, 4], BF16, name="grouped_out%d" % i, tag="grouped_out", bufs=8, align_bytes=64)
+            dst = grouped["out", i][:, g, :, :].rearrange("p m j -> p (m j)").bitcast(F32).rearrange("p (m u) -> p m u", u=2)
+            copy(eng, dst, turned["out", i, g][:].rearrange("p u m -> p m u"))
+
+        mag = keep.tile([P, P + 8], F32, name="mag")
+        dec = keep.tile([P, P + 8], F32, name="dec")
+        logc = keep.tile([P, P + 8], F32, name="logc")
+        td32 = keep.tile([P, P], F32, name="td32")
+        log_t = keep.tile([P, N], F32, name="log_t")
+        log_td = keep.tile([P, TILES], F32, name="log_td")
+        peak = keep.tile([P, TILES], F32, name="peak")
+        spread = {}
+
+        def spread_turn(h):
+            spread[h] = psum.tile([P, 4, P], F32, name="spread%d" % h, tag="acc_fm")
+            for j in range(4):
+                nc.tensor.transpose(spread[h][:, j, :], logc[:, P + 4 * h + j : P + 4 * h + j + 1].to_broadcast([P, P]), ident[:])
+
+        def spread_copy(eng, h):
+            copy(eng, log_t[:, HALF * h : HALF * (h + 1)].rearrange("p (q j) -> p q j", j=4), spread[h][:].rearrange("p j q -> p q j"))
+
+        nc.vector.memset(times[:, 0:P], 0.0)
+        nc.vector.memset(warm[:], 0.0)
+        make_identity(nc, ident[:])
+        nc.sync.dma_start(out=times[0:TILES, 0:P], in_=td.rearrange("(i q) -> i q", q=P))
+        nc.vector.tensor_copy(out=td32[:], in_=times[:, 0:P])
+        nc.sync.dma_start(out=times[:, P : P + 8].rearrange("p (h j) -> p h j", h=2), in_=t.rearrange("(h p j) -> p h j", h=2, j=4))
+        load_w("r", 0, 0)
+        interleave("v", "r", 0, 0, 0, 256)
+        interleave("v", "r", 0, 0, 256, 512)
+        quant_w("r", 0, 0)
+        nc.scalar.activation(out=warm[:, 0:1], in_=warm[:, 1:2], func=ACT.Exp)
+        nc.scalar.activation(out=mag[:], in_=times[:, 0 : P + 8], func=ACT.Abs, scale=4.0)
+        nc.scalar.activation(out=dec[:], in_=mag[:], func=ACT.Exp, scale=-2.0)
+        nc.scalar.activation(out=dec[:], in_=dec[:], func=ACT.Ln, bias=1.0)
+        nc.vector.tensor_tensor(out=logc[:], in0=mag[:], in1=dec[:], op=ALU.add)
+        nc.scalar.activation(out=warm[:, 2:3], in_=warm[:, 1:2], func=ACT.Sigmoid)
+        spread_turn(0)
+        spread_turn(1)
+        spread_copy("s", 0)
+        load_w("r", 1, 1)
+        load_f(0)
+        load_w("r", 1, 0)
+        load_w("r", 0, 1)
+        load_f(1)
+        load_f(2)
+        load_w("c", 1, 1)
+        load_f(3)
+        load_w("c", 0, 0)
+        load_f(4)
+        small = psum.tile([P, 2, P], F32, name="small", tag="turned", bufs=4)
+        nc.tensor.transpose(small[:, 0, :], logc[:, 0:P], ident[:])
+        nc.tensor.transpose(small[:, 1, :], td32[:], ident[:])
+        nc.scalar.activation(out=peak[:], in_=small[:, 1, 0:TILES], func=ACT.Sigmoid, scale=8.0)
+        nc.scalar.copy(out=log_td[:], in_=small[:, 0, 0:TILES])
+        load_f(5)
+        load_w("c", 0, 1)
+        load_w("c", 1, 0)
+        load_f(6)
+        load_f(7)
+        load_fd(0)
+        load_fd(1)
+        load_fd(2)
+        load_fd(3)
+        load_fd(4)
+        load_fd(5)
+        load_fd(6)
+        load_fd(7)
+        interleave("v", "r", 1, 1, 0, 256)
+        interleave("v", "r", 1, 1, 256, 512)
+        interleave("v", "r", 1, 0, 0, 256)
+        interleave("v", "r", 1, 0, 256, 512)
+        quant_w("r", 1, 0)
+        turn("f", 0)
+        gather("s", "f", 0)
+        quant("f", 0)
+        spread_copy("s", 1)
+        quant_w("r", 1, 1)
+        turn("f", 1)
+        interleave("v", "r", 0, 1, 0, 256)
+        interleave("s", "r", 0, 1, 256, 512)
+        quant_w("r", 0, 1)
+        gather("s", "f", 1)
+        quant("f", 1)
+        turn("f", 2)
+        gather("s", "f", 2)
+        quant("f", 2)
+        multiply("f", 0, 0)
+        interleave("s", "c", 1, 1, 0, 256)
+        interleave("v", "c", 1, 1, 256, 512)
+        quant_w("c", 1, 1)
+        turn("f", 3)
+        multiply("f", 0, 1)
+        window(0)
+        windowed("f", 0, 0)
+        windowed("f", 0, 1)
+        turn("f", 4)
+        gather("s", "f", 3)
+        quant("f", 3)
+        multiply("f", 1, 0)
+        turn("fm", 0)
+        multiply("f", 1, 1)
+        turn("f", 5)
+        interleave("s", "c", 0, 0, 0, 256)
+        interleave("v", "c", 0, 0, 256, 512)
+        quant_w("c", 0, 0)
+        window(1)
+        windowed("f", 1, 0)
+        windowed("f", 1, 1)
+        gather("s", "fm", 0)
+        quant("fm", 0)
+        gather("s", "f", 4)
+        quant("f", 4)
+        multiply("f", 2, 0)
+        turn("f", 6)
+        turn("fm", 1)
+        interleave("s", "c", 0, 1, 0, 256)
+        interleave("v", "c", 0, 1, 256, 512)
+        quant_w("c", 0, 1)
+        multiply("f", 2, 1)
+        interleave("s", "c", 1, 0, 0, 256)
+        interleave("v", "c", 1, 0, 256, 512)
+        quant_w("c", 1, 0)
+        window(2)
+        windowed("f", 2, 0)
+        windowed("f", 2, 1)
+        gather("s", "f", 5)
+        quant("f", 5)
+        multiply("fm", 0, 1)
+        turn("f", 7)
+        gather("s", "fm", 1)
+        quant("fm", 1)
+        multiply("fm", 0, 0)
+        windowed("fm", 0, 0)
+        windowed("fm", 0, 1)
+        add_direct(nc.gpsimd, 0, 1)
+        store_res(0, 512, 1024)
+        multiply("f", 3, 0)
+        add_direct(nc.gpsimd, 0, 0)
+        store_res(0, 0, 512)
+        turn("fm", 2)
+        multiply("f", 3, 1)
+        gather("s", "f", 6)
+        quant("f", 6)
+        window(3)
+        windowed("f", 3, 0)
+        windowed("f", 3, 1)
+        multiply("fm", 1, 1)
+        gather("s", "fm", 2)
+        quant("fm", 2)
+        multiply("fm", 1, 0)
+        windowed("fm", 1, 0)
+        windowed("fm", 1, 1)
+        add_direct(nc.gpsimd, 1, 1)
+        store_res(1, 512, 1024)
+        multiply("f", 4, 0)
+        add_direct(nc.gpsimd, 1, 0)
+        store_res(1, 0, 512)
+        turn("fm", 3)
+        gather("s", "f", 7)
+        quant("f", 7)
+        multiply("f", 4, 1)
+        window(4)
+        windowed("f", 4, 0)
+        windowed("f", 4, 1)
+        gather("s", "fm", 3)
+        quant("fm", 3)
+        multiply("fm", 2, 1)
+        multiply("fm", 2, 0)
+        windowed("fm", 2, 0)
+        windowed("fm", 2, 1)
+        multiply("f", 5, 0)
+        add_direct(nc.gpsimd, 2, 1)
+        store_res(2, 512, 1024)
+        add_direct(nc.vector, 2, 0)
+        store_res(2, 0, 512)
+        turn("fm", 4)
+        cast("s", 0, 0)
+        cast("s", 0, 1)
+        turn("out", 0)
+        window(5)
+        windowed("f", 5, 0)
+        multiply("f", 5, 1)
+        windowed("f", 5, 1)
+        gather("s", "fm", 4)
+        quant("fm", 4)
+        multiply("fm", 3, 1)
+        multiply("fm", 3, 0)
+        windowed("fm", 3, 0)
+        windowed("fm", 3, 1)
+        multiply("f", 6, 0)
+        add_direct(nc.gpsimd, 3, 1)
+        store_res(3, 512, 1024)
+        add_direct(nc.gpsimd, 3, 0)
+        store_res(3, 0, 512)
+        turn("fm", 5)
+        cast("s", 1, 0)
+        cast("s", 1, 1)
+        turn("out", 1)
+        window(6)
+        windowed("f", 6, 0)
+        gather("s", "out", 0)
+        multiply("f", 6, 1)
+        windowed("f", 6, 1)
+        gather("s", "fm", 5)
+        quant("fm", 5)
+        multiply("fm", 4, 0)
+        windowed("fm", 4, 0)
+        multiply("fm", 4, 1)
+        windowed("fm", 4, 1)
+        multiply("f", 7, 0)
+        add_direct(nc.gpsimd, 4, 0)
+        store_res(4, 0, 512)
+        add_direct(nc.gpsimd, 4, 1)
+        store_res(4, 512, 1024)
+        turn("fm", 6)
+        window(7)
+        windowed("f", 7, 0)
+        cast("s", 2, 0)
+        cast("s", 2, 1)
+        multiply("f", 7, 1)
+        windowed("f", 7, 1)
+        gather("s", "fm", 6)
+        quant("fm", 6)
+        multiply("fm", 5, 0)
+        windowed("fm", 5, 0)
+        multiply("fm", 5, 1)
+        windowed("fm", 5, 1)
+        add_direct(nc.vector, 5, 0)
+        store_res(5, 0, 512)
+        turn("fm", 7)
+        add_direct(nc.gpsimd, 5, 1)
+        store_res(5, 512, 1024)
+        gather("s", "out", 1)
+        cast("s", 3, 0)
+        cast("s", 3, 1)
+        gather("s", "fm", 7)
+        quant("fm", 7)
+        turn("out", 2)
+        multiply("fm", 6, 0)
+        windowed("fm", 6, 0)
+        multiply("fm", 6, 1)
+        windowed("fm", 6, 1)
+        add_direct(nc.vector, 6, 0)
+        store_res(6, 0, 512)
+        add_direct(nc.gpsimd, 6, 1)
+        store_res(6, 512, 1024)
+        cast("s", 4, 0)
+        cast("s", 4, 1)
+        multiply("fm", 7, 0)
+        windowed("fm", 7, 0)
+        multiply("fm", 7, 1)
+        windowed("fm", 7, 1)
+        add_direct(nc.vector, 7, 0)
+        store_res(7, 0, 512)
+        gather("s", "out", 2)
+        add_direct(nc.vector, 7, 1)
+        store_res(7, 512, 1024)
+        cast("s", 5, 0)
+        cast("s", 5, 1)
+        quant_out(0, 0)
+        quant_out(0, 1)
+        turn("out", 3)
+        cast("s", 6, 0)
+        cast("s", 6, 1)
+        gather("s", "out", 3)
+        quant_out(1, 0)
+        quant_out(1, 1)
+        quant_out(2, 0)
+        quant_out(2, 1)
+        quant_out(3, 0)
+        quant_out(3, 1)
+        cast("v", 7, 0)
+        cast("v", 7, 1)
+        turn("out", 4)
+        gather("s", "out", 4)
+        quant_out(4, 0)
+        quant_out(4, 1)
+        turn("out", 5)
+        gather("s", "out", 5)
+        quant_out(5, 0)
+        quant_out(5, 1)
+        turn("out", 6)
+        gather("s", "out", 6)
+        quant_out(6, 0)
+        quant_out(6, 1)
+        turn_half(7, 0)
+        gather_half("s", 7, 0)
+        quant_out(7, 0)
+        turn_half(7, 1)
+        gather_half("v", 7, 1)
+        quant_out(7, 1)
+        store_words(0)
+        store_words(1)
+        store_scales(0)
+        store_words(2)
+        store_words(3)
+        store_scales(1)

@@ -16,8 +16,8 @@ P = 128
 N = 1024
 TILES = 8
 HALF = 512
-WORD_GROUPS = ((0, 2), (2, 4), (4, 7), (7, 8))
-SCALE_GROUPS = ((0, 5), (5, 8))
+WORD_GROUPS = ((0, 2), (2, 4), (4, 6), (6, 7), (7, 8))
+SCALE_GROUPS = ((0, 6), (6, 8))
 FLOPS = 2 * 2 * N * N * N
 
 
@@ -30,7 +30,7 @@ def tile_marchenkofocusingiteration_x1_kernel(tc, f, r, c, fd, td, t, out_0, out
         ctx.enter_context(tc.manual_schedule())
 
         ident = keep.tile([P, P], F32, name="ident")
-        times = keep.tile([P, P + 16], BF16, name="times")
+        times = keep.tile([P, 16 + P + 8], BF16, name="times")
         warm = keep.tile([P, 8], F32, name="warm")
         raw = {}
         grouped = {}
@@ -48,10 +48,12 @@ def tile_marchenkofocusingiteration_x1_kernel(tc, f, r, c, fd, td, t, out_0, out
         out_scales = {}
         weights = {"r": r, "c": c}
 
-        def load_w(w, g, h):
-            raw[w, g, h] = keep.tile([P, 4, HALF], BF16, name="raw_%s%d%d" % (w, g, h))
-            rows = weights[w][512 * g : 512 * (g + 1), HALF * h : HALF * (h + 1)]
-            nc.sync.dma_start(out=raw[w, g, h][:], in_=rows.rearrange("(p j) n -> p j n", j=4))
+        def load_w(w, g, lo, hi):
+            tile = keep.tile([P, 4, hi - lo], BF16, name="raw_%s%d_%d" % (w, g, lo))
+            for col in range(lo, hi, 256):
+                raw[w, g, col] = tile[:, :, col - lo : col - lo + 256]
+            rows = weights[w][512 * g : 512 * (g + 1), lo:hi]
+            nc.sync.dma_start(out=tile[:], in_=rows.rearrange("(p j) n -> p j n", j=4))
 
         def load_f(i):
             f_rows[i] = keep.tile([P, N], BF16, name="f_rows%d" % i)
@@ -65,7 +67,7 @@ def tile_marchenkofocusingiteration_x1_kernel(tc, f, r, c, fd, td, t, out_0, out
             if (w, g, h) not in grouped:
                 grouped[w, g, h] = work.tile([P, HALF, 4], BF16, name="grouped_%s%d%d" % (w, g, h), tag="wgrouped", bufs=4, align_bytes=64)
             dst = grouped[w, g, h][:, lo:hi, :].rearrange("p (n i) j -> p n j i", i=4)
-            src = raw[w, g, h][:, :, lo:hi].rearrange("p j (n i) -> p n j i", i=4)
+            src = raw[w, g, HALF * h + lo].rearrange("p j (n i) -> p n j i", i=4)
             if eng == "v":
                 nc.vector.tensor_copy(out=dst, in_=src)
             else:
@@ -95,9 +97,24 @@ def tile_marchenkofocusingiteration_x1_kernel(tc, f, r, c, fd, td, t, out_0, out
                 nc.scalar.copy(out=out, in_=in_)
 
         def gather(eng, kind, i):
-            grouped[kind, i] = work.tile([P, 2, P, 4], BF16, name="grouped_%s%d" % (kind, i), tag="grouped_" + kind, bufs=8 if kind == "out" else 3, align_bytes=64)
+            grouped[kind, i] = work.tile([P, 2, P, 4], BF16, name="grouped_%s%d" % (kind, i), tag="grouped_" + kind, bufs=3, align_bytes=64)
             dst = grouped[kind, i][:].rearrange("p g m j -> p (g m j)").bitcast(F32).rearrange("p (g m u) -> p g m u", g=2, u=2)
             copy(eng, dst, turned[kind, i][:].rearrange("p g u m -> p g m u"))
+
+        def gather_out(eng, i, g_lo, g_hi):
+            lo, hi = group_of(WORD_GROUPS, i)
+            if ("out", lo) not in grouped:
+                grouped["out", lo] = keep.tile([P, 2, P * (hi - lo), 4], BF16, name="grouped_out%d" % lo, align_bytes=64)
+            dst = grouped["out", lo][:, g_lo:g_hi, P * (i - lo) : P * (i - lo + 1), :].rearrange("p g m j -> p g (m j)").bitcast(F32)
+            copy(eng, dst.rearrange("p g (m u) -> p g m u", u=2), turned["out", i, g_lo][:].rearrange("p g u m -> p g m u"))
+
+        def turn_out(i, g_lo, g_hi):
+            src = res16[i][:].bitcast(F32)
+            bank = psum.tile([P, g_hi - g_lo, 2, P], F32, name="turned_out%d%d" % (i, g_lo), tag="turned", bufs=4)
+            turned["out", i, g_lo] = bank
+            for g in range(g_lo, g_hi):
+                for u in range(2):
+                    nc.tensor.transpose(bank[:, g - g_lo, u, :], src[:, 256 * g + P * u : 256 * g + P * (u + 1)], ident[:])
 
         def quant(kind, i):
             codes[kind, i] = work.tile([P, 2 * P], U32, name="codes_%s%d" % (kind, i), tag="codes_" + kind, bufs=4, align_bytes=64)
@@ -162,9 +179,9 @@ def tile_marchenkofocusingiteration_x1_kernel(tc, f, r, c, fd, td, t, out_0, out
             if (s_lo, s_hi) not in out_scales:
                 out_scales[s_lo, s_hi] = keep.tile([P, 2, P * (s_hi - s_lo)], U8, name="out_scales%d" % s_lo, align_bytes=64)
             nc.vector.quantize_mx(
-                out=words[lo, hi][:, g, P * (i - lo) : P * (i - lo + 1)].bitcast(FP8X4),
-                scales=out_scales[s_lo, s_hi][:, g, P * (i - s_lo) : P * (i - s_lo + 1)],
-                in_=grouped["out", i][:, g, :, :].rearrange("p m j -> p (m j)"),
+                out=words[lo, hi][:, g, :].bitcast(FP8X4),
+                scales=out_scales[s_lo, s_hi][:, g, P * (lo - s_lo) : P * (hi - s_lo)],
+                in_=grouped["out", lo][:, g, :, :].rearrange("p m j -> p (m j)"),
             )
 
         def store_words(k):
@@ -219,280 +236,274 @@ def tile_marchenkofocusingiteration_x1_kernel(tc, f, r, c, fd, td, t, out_0, out
         def spread_copy(eng, h):
             copy(eng, log_t[:, HALF * h : HALF * (h + 1)].rearrange("p (q j) -> p q j", j=4), spread[h][:].rearrange("p j q -> p q j"))
 
-        nc.vector.memset(times[:, 0:P], 0.0)
-        nc.vector.memset(warm[:], 0.0)
-        make_identity(nc, ident[:])
-        nc.sync.dma_start(out=times[0:TILES, 0:P], in_=td.rearrange("(i q) -> i q", q=P))
-        nc.vector.tensor_copy(out=td32[:], in_=times[:, 0:P])
-        nc.sync.dma_start(out=times[:, P : P + 8].rearrange("p (h j) -> p h j", h=2), in_=t.rearrange("(h p j) -> p h j", h=2, j=4))
-        load_w("r", 0, 0)
+        nc.gpsimd.memset(times[:, 0 : 16 + P], 0.0)
+        load_w("r", 0, 0, 256)
         interleave("v", "r", 0, 0, 0, 256)
+        make_identity(nc, ident[:])
+        nc.sync.dma_start(out=times[:, 16 + P :].rearrange("p (h j) -> p h j", h=2), in_=t.rearrange("(h p j) -> p h j", h=2, j=4))
+        nc.sync.dma_start(out=times[0:TILES, 16 : 16 + P], in_=td.rearrange("(i q) -> i q", q=P))
+        nc.vector.tensor_copy(out=td32[:], in_=times[:, 16 : 16 + P])
+        load_w("r", 0, 256, 512)
         interleave("v", "r", 0, 0, 256, 512)
         quant_w("r", 0, 0)
-        nc.scalar.activation(out=warm[:, 0:1], in_=warm[:, 1:2], func=ACT.Exp)
-        nc.scalar.activation(out=mag[:], in_=times[:, 0 : P + 8], func=ACT.Abs, scale=4.0)
+        load_w("r", 1, 512, 1024)
+        interleave("v", "r", 1, 1, 0, 256)
+        interleave("v", "r", 1, 1, 256, 512)
+        nc.scalar.activation(out=warm[:, 0:1], in_=times[:, 0:1], func=ACT.Exp)
+        nc.scalar.activation(out=mag[:], in_=times[:, 16:], func=ACT.Abs, scale=4.0)
         nc.scalar.activation(out=dec[:], in_=mag[:], func=ACT.Exp, scale=-2.0)
         nc.scalar.activation(out=dec[:], in_=dec[:], func=ACT.Ln, bias=1.0)
         nc.vector.tensor_tensor(out=logc[:], in0=mag[:], in1=dec[:], op=ALU.add)
-        nc.scalar.activation(out=warm[:, 2:3], in_=warm[:, 1:2], func=ACT.Sigmoid)
-        spread_turn(0)
-        spread_turn(1)
-        spread_copy("s", 0)
-        load_w("r", 1, 1)
-        load_f(0)
-        load_w("r", 1, 0)
-        load_w("r", 0, 1)
-        load_f(1)
-        load_f(2)
-        load_w("c", 1, 1)
-        load_f(3)
-        load_w("c", 0, 0)
-        load_f(4)
         small = psum.tile([P, 2, P], F32, name="small", tag="turned", bufs=4)
         nc.tensor.transpose(small[:, 0, :], logc[:, 0:P], ident[:])
         nc.tensor.transpose(small[:, 1, :], td32[:], ident[:])
+        spread_turn(0)
+        spread_turn(1)
         nc.scalar.activation(out=peak[:], in_=small[:, 1, 0:TILES], func=ACT.Sigmoid, scale=8.0)
         nc.scalar.copy(out=log_td[:], in_=small[:, 0, 0:TILES])
-        load_f(5)
-        load_w("c", 0, 1)
-        load_w("c", 1, 0)
-        load_f(6)
-        load_f(7)
-        load_fd(0)
-        load_fd(1)
-        load_fd(2)
-        load_fd(3)
-        load_fd(4)
-        load_fd(5)
-        load_fd(6)
-        load_fd(7)
-        interleave("v", "r", 1, 1, 0, 256)
-        interleave("v", "r", 1, 1, 256, 512)
+        spread_copy("s", 1)
+        load_w("r", 0, 512, 1024)
+        interleave("v", "r", 0, 1, 0, 256)
+        interleave("v", "r", 0, 1, 256, 512)
+        load_w("r", 1, 0, 512)
         interleave("v", "r", 1, 0, 0, 256)
         interleave("v", "r", 1, 0, 256, 512)
-        quant_w("r", 1, 0)
-        turn("f", 0)
-        gather("s", "f", 0)
-        quant("f", 0)
-        spread_copy("s", 1)
         quant_w("r", 1, 1)
-        turn("f", 1)
-        interleave("v", "r", 0, 1, 0, 256)
-        interleave("s", "r", 0, 1, 256, 512)
         quant_w("r", 0, 1)
+        quant_w("r", 1, 0)
+        spread_copy("s", 0)
+        window(0)
+        load_w("c", 0, 0, 512)
+        interleave("v", "c", 0, 0, 0, 256)
+        interleave("v", "c", 0, 0, 256, 512)
+        load_f(0)
+        load_f(1)
+        turn("f", 0)
+        load_f(2)
+        gather("s", "f", 0)
+        turn("f", 1)
+        load_f(3)
+        quant("f", 0)
         gather("s", "f", 1)
-        quant("f", 1)
         turn("f", 2)
+        load_f(4)
+        quant("f", 1)
+        turn("f", 3)
+        turn("f", 4)
+        quant_w("c", 0, 0)
         gather("s", "f", 2)
         quant("f", 2)
-        multiply("f", 0, 0)
-        interleave("s", "c", 1, 1, 0, 256)
-        interleave("v", "c", 1, 1, 256, 512)
-        quant_w("c", 1, 1)
-        turn("f", 3)
-        multiply("f", 0, 1)
-        window(0)
-        windowed("f", 0, 0)
-        windowed("f", 0, 1)
-        turn("f", 4)
         gather("s", "f", 3)
         quant("f", 3)
-        multiply("f", 1, 0)
-        turn("fm", 0)
-        multiply("f", 1, 1)
-        turn("f", 5)
-        interleave("s", "c", 0, 0, 0, 256)
-        interleave("v", "c", 0, 0, 256, 512)
-        quant_w("c", 0, 0)
+        multiply("f", 0, 0)
+        windowed("f", 0, 0)
+        multiply("f", 0, 1)
+        windowed("f", 0, 1)
         window(1)
-        windowed("f", 1, 0)
-        windowed("f", 1, 1)
-        gather("s", "fm", 0)
-        quant("fm", 0)
         gather("s", "f", 4)
         quant("f", 4)
-        multiply("f", 2, 0)
-        turn("f", 6)
-        turn("fm", 1)
+        load_f(5)
+        turn("f", 5)
+        load_w("c", 0, 512, 1024)
         interleave("s", "c", 0, 1, 0, 256)
         interleave("v", "c", 0, 1, 256, 512)
-        quant_w("c", 0, 1)
-        multiply("f", 2, 1)
-        interleave("s", "c", 1, 0, 0, 256)
-        interleave("v", "c", 1, 0, 256, 512)
-        quant_w("c", 1, 0)
-        window(2)
-        windowed("f", 2, 0)
-        windowed("f", 2, 1)
         gather("s", "f", 5)
+        multiply("f", 1, 0)
+        windowed("f", 1, 0)
+        multiply("f", 1, 1)
+        windowed("f", 1, 1)
+        load_w("c", 1, 0, 512)
+        interleave("v", "c", 1, 0, 0, 256)
+        interleave("s", "c", 1, 0, 256, 512)
         quant("f", 5)
-        multiply("fm", 0, 1)
-        turn("f", 7)
+        quant_w("c", 1, 0)
+        turn("fm", 0)
+        gather("s", "fm", 0)
+        quant("fm", 0)
+        window(2)
+        load_f(6)
+        turn("f", 6)
+        gather("s", "f", 6)
+        quant_w("c", 0, 1)
+        load_fd(0)
+        multiply("f", 2, 0)
+        windowed("f", 2, 0)
+        multiply("f", 2, 1)
+        windowed("f", 2, 1)
+        turn("fm", 1)
+        quant("f", 6)
         gather("s", "fm", 1)
         quant("fm", 1)
+        window(3)
+        load_f(7)
+        turn("f", 7)
+        gather("s", "f", 7)
+        load_fd(1)
         multiply("fm", 0, 0)
         windowed("fm", 0, 0)
-        windowed("fm", 0, 1)
-        add_direct(nc.gpsimd, 0, 1)
-        store_res(0, 512, 1024)
+        load_w("c", 1, 512, 1024)
+        interleave("v", "c", 1, 1, 0, 256)
         multiply("f", 3, 0)
-        add_direct(nc.gpsimd, 0, 0)
-        store_res(0, 0, 512)
-        turn("fm", 2)
-        multiply("f", 3, 1)
-        gather("s", "f", 6)
-        quant("f", 6)
-        window(3)
         windowed("f", 3, 0)
+        multiply("f", 3, 1)
         windowed("f", 3, 1)
-        multiply("fm", 1, 1)
+        turn("fm", 2)
+        interleave("s", "c", 1, 1, 256, 512)
+        quant_w("c", 1, 1)
+        quant("f", 7)
         gather("s", "fm", 2)
         quant("fm", 2)
+        load_fd(2)
+        window(4)
         multiply("fm", 1, 0)
         windowed("fm", 1, 0)
-        windowed("fm", 1, 1)
-        add_direct(nc.gpsimd, 1, 1)
-        store_res(1, 512, 1024)
+        add_direct(nc.gpsimd, 0, 0)
+        store_res(0, 0, 512)
+        cast("s", 0, 0)
         multiply("f", 4, 0)
-        add_direct(nc.gpsimd, 1, 0)
-        store_res(1, 0, 512)
-        turn("fm", 3)
-        gather("s", "f", 7)
-        quant("f", 7)
-        multiply("f", 4, 1)
-        window(4)
         windowed("f", 4, 0)
+        multiply("f", 4, 1)
         windowed("f", 4, 1)
+        turn("fm", 3)
+        load_fd(3)
+        multiply("fm", 0, 1)
+        windowed("fm", 0, 1)
         gather("s", "fm", 3)
         quant("fm", 3)
-        multiply("fm", 2, 1)
+        window(5)
         multiply("fm", 2, 0)
         windowed("fm", 2, 0)
-        windowed("fm", 2, 1)
+        add_direct(nc.gpsimd, 1, 0)
+        store_res(1, 0, 512)
+        cast("s", 1, 0)
         multiply("f", 5, 0)
-        add_direct(nc.gpsimd, 2, 1)
-        store_res(2, 512, 1024)
-        add_direct(nc.vector, 2, 0)
-        store_res(2, 0, 512)
-        turn("fm", 4)
-        cast("s", 0, 0)
-        cast("s", 0, 1)
-        turn("out", 0)
-        window(5)
         windowed("f", 5, 0)
         multiply("f", 5, 1)
         windowed("f", 5, 1)
+        turn("fm", 4)
+        load_fd(4)
+        multiply("fm", 1, 1)
+        windowed("fm", 1, 1)
+        add_direct(nc.gpsimd, 0, 1)
+        store_res(0, 512, 1024)
+        window(6)
         gather("s", "fm", 4)
         quant("fm", 4)
-        multiply("fm", 3, 1)
         multiply("fm", 3, 0)
         windowed("fm", 3, 0)
-        windowed("fm", 3, 1)
+        add_direct(nc.gpsimd, 2, 0)
+        store_res(2, 0, 512)
         multiply("f", 6, 0)
-        add_direct(nc.gpsimd, 3, 1)
-        store_res(3, 512, 1024)
-        add_direct(nc.gpsimd, 3, 0)
-        store_res(3, 0, 512)
-        turn("fm", 5)
-        cast("s", 1, 0)
-        cast("s", 1, 1)
-        turn("out", 1)
-        window(6)
         windowed("f", 6, 0)
-        gather("s", "out", 0)
         multiply("f", 6, 1)
         windowed("f", 6, 1)
+        turn("fm", 5)
+        load_fd(5)
+        multiply("fm", 2, 1)
+        windowed("fm", 2, 1)
+        add_direct(nc.gpsimd, 1, 1)
+        store_res(1, 512, 1024)
+        window(7)
+        add_direct(nc.gpsimd, 3, 0)
+        store_res(3, 0, 512)
+        multiply("f", 7, 0)
+        multiply("fm", 4, 0)
+        windowed("f", 7, 0)
+        multiply("f", 7, 1)
+        windowed("fm", 4, 0)
+        windowed("f", 7, 1)
         gather("s", "fm", 5)
         quant("fm", 5)
-        multiply("fm", 4, 0)
-        windowed("fm", 4, 0)
+        load_fd(6)
+        multiply("fm", 3, 1)
+        windowed("fm", 3, 1)
+        turn("fm", 6)
+        add_direct(nc.gpsimd, 2, 1)
+        store_res(2, 512, 1024)
+        cast("s", 2, 0)
+        cast("s", 0, 1)
+        turn_out(0, 0, 2)
+        add_direct(nc.vector, 4, 0)
+        store_res(4, 0, 512)
+        add_direct(nc.gpsimd, 3, 1)
+        store_res(3, 512, 1024)
+        load_fd(7)
         multiply("fm", 4, 1)
         windowed("fm", 4, 1)
-        multiply("f", 7, 0)
-        add_direct(nc.gpsimd, 4, 0)
-        store_res(4, 0, 512)
-        add_direct(nc.gpsimd, 4, 1)
-        store_res(4, 512, 1024)
-        turn("fm", 6)
-        window(7)
-        windowed("f", 7, 0)
-        cast("s", 2, 0)
-        cast("s", 2, 1)
-        multiply("f", 7, 1)
-        windowed("f", 7, 1)
-        gather("s", "fm", 6)
-        quant("fm", 6)
         multiply("fm", 5, 0)
         windowed("fm", 5, 0)
-        multiply("fm", 5, 1)
-        windowed("fm", 5, 1)
+        turn("fm", 7)
+        gather("s", "fm", 6)
+        quant("fm", 6)
+        cast("s", 1, 1)
+        turn_out(1, 0, 2)
+        add_direct(nc.vector, 4, 1)
+        store_res(4, 512, 1024)
         add_direct(nc.vector, 5, 0)
         store_res(5, 0, 512)
-        turn("fm", 7)
-        add_direct(nc.gpsimd, 5, 1)
-        store_res(5, 512, 1024)
-        gather("s", "out", 1)
-        cast("s", 3, 0)
-        cast("s", 3, 1)
+        multiply("fm", 5, 1)
+        windowed("fm", 5, 1)
+        cast("s", 2, 1)
+        turn_out(2, 0, 2)
+        multiply("fm", 6, 0)
+        gather_out("s", 0, 0, 2)
         gather("s", "fm", 7)
         quant("fm", 7)
-        turn("out", 2)
-        multiply("fm", 6, 0)
         windowed("fm", 6, 0)
+        add_direct(nc.gpsimd, 5, 1)
+        store_res(5, 512, 1024)
         multiply("fm", 6, 1)
         windowed("fm", 6, 1)
         add_direct(nc.vector, 6, 0)
         store_res(6, 0, 512)
+        cast("s", 3, 0)
+        cast("s", 3, 1)
+        turn_out(3, 0, 2)
         add_direct(nc.gpsimd, 6, 1)
         store_res(6, 512, 1024)
-        cast("s", 4, 0)
-        cast("s", 4, 1)
         multiply("fm", 7, 0)
-        windowed("fm", 7, 0)
         multiply("fm", 7, 1)
+        windowed("fm", 7, 0)
         windowed("fm", 7, 1)
         add_direct(nc.vector, 7, 0)
         store_res(7, 0, 512)
-        gather("s", "out", 2)
         add_direct(nc.vector, 7, 1)
-        store_res(7, 512, 1024)
-        cast("s", 5, 0)
-        cast("s", 5, 1)
-        quant_out(0, 0)
-        quant_out(0, 1)
-        turn("out", 3)
-        cast("s", 6, 0)
-        cast("s", 6, 1)
-        gather("s", "out", 3)
+        gather_out("s", 1, 0, 2)
         quant_out(1, 0)
         quant_out(1, 1)
-        quant_out(2, 0)
-        quant_out(2, 1)
+        store_res(7, 512, 1024)
+        store_words(0)
+        cast("s", 4, 0)
+        cast("s", 4, 1)
+        gather_out("s", 2, 0, 2)
+        turn_out(4, 0, 2)
+        cast("s", 5, 0)
+        cast("s", 5, 1)
+        gather_out("s", 3, 0, 2)
         quant_out(3, 0)
         quant_out(3, 1)
-        cast("v", 7, 0)
+        store_words(1)
+        cast("s", 6, 0)
+        cast("s", 6, 1)
+        gather_out("s", 4, 0, 2)
+        turn_out(5, 0, 2)
+        turn_out(6, 0, 2)
+        gather_out("s", 5, 0, 2)
+        cast("s", 7, 0)
         cast("v", 7, 1)
-        turn("out", 4)
-        gather("s", "out", 4)
-        quant_out(4, 0)
-        quant_out(4, 1)
-        turn("out", 5)
-        gather("s", "out", 5)
         quant_out(5, 0)
         quant_out(5, 1)
-        turn("out", 6)
-        gather("s", "out", 6)
+        store_words(2)
+        store_scales(0)
+        gather_out("s", 6, 0, 2)
         quant_out(6, 0)
         quant_out(6, 1)
-        turn_half(7, 0)
-        gather_half("s", 7, 0)
-        quant_out(7, 0)
-        turn_half(7, 1)
-        gather_half("v", 7, 1)
-        quant_out(7, 1)
-        store_words(0)
-        store_words(1)
-        store_scales(0)
-        store_words(2)
         store_words(3)
+        turn_out(7, 0, 1)
+        gather_out("v", 7, 0, 1)
+        turn_out(7, 1, 2)
+        quant_out(7, 0)
+        gather_out("s", 7, 1, 2)
+        quant_out(7, 1)
+        store_words(4)
         store_scales(1)

from contextlib import ExitStack

import concourse.mybir as mybir
from concourse.masks import make_identity

F32 = mybir.dt.float32
BF16 = mybir.dt.bfloat16
I32 = mybir.dt.int32
U32 = mybir.dt.uint32
U8 = mybir.dt.uint8
FP8X4 = mybir.dt.float8_e4m3fn_x4
ACT = mybir.ActivationFunctionType
ALU = mybir.AluOpType

P = 128
N = 1024
TILES = 8
HALF = 512
WORD_GROUPS = ((0, 2), (2, 4), (4, 6), (6, 7), (7, 8))
SCALE_GROUPS = ((0, 6), (6, 8))
FLOPS = 2 * 2 * N * N * N


def tile_marchenkofocusingiteration_x1_kernel(tc, f, r, c, fd, td, t, out_0, out_1, out_2):
    nc = tc.nc
    with ExitStack() as ctx:
        keep = ctx.enter_context(tc.tile_pool(name="keep", bufs=1))
        work = ctx.enter_context(tc.tile_pool(name="work", bufs=3))
        psum = ctx.enter_context(tc.psum_pool(name="psum", bufs=2))
        ctx.enter_context(tc.manual_schedule())

        ident = keep.tile([P, P], F32, name="ident")
        times = keep.tile([P, 16 + P + 8], BF16, name="times")
        warm = keep.tile([P, 8], F32, name="warm")
        raw = {}
        grouped = {}
        codes = {}
        scales = {}
        f_rows = {}
        fd_rows = {}
        sig = {}
        acc = {}
        fm = {}
        turned = {}
        res = {}
        res16 = {}
        words = {}
        out_scales = {}
        weights = {"r": r, "c": c}

        def load_w(w, g, lo, hi):
            tile = keep.tile([P, 4, hi - lo], BF16, name="raw_%s%d_%d" % (w, g, lo))
            for col in range(lo, hi, 256):
                raw[w, g, col] = tile[:, :, col - lo : col - lo + 256]
            rows = weights[w][512 * g : 512 * (g + 1), lo:hi]
            nc.sync.dma_start(out=tile[:], in_=rows.rearrange("(p j) n -> p j n", j=4))

        def load_f(i):
            f_rows[i] = keep.tile([P, N], BF16, name="f_rows%d" % i)
            nc.sync.dma_start(out=f_rows[i][:], in_=f[P * i : P * (i + 1), :])

        def load_fd(i):
            fd_rows[i] = keep.tile([P, N], BF16, name="fd_rows%d" % i)
            nc.sync.dma_start(out=fd_rows[i][:], in_=fd[P * i : P * (i + 1), :])

        def interleave(eng, w, g, h, lo, hi):
            if (w, g, h) not in grouped:
                grouped[w, g, h] = work.tile([P, HALF, 4], BF16, name="grouped_%s%d%d" % (w, g, h), tag="wgrouped", bufs=4, align_bytes=64)
            dst = grouped[w, g, h][:, lo:hi, :].rearrange("p (n i) j -> p n j i", i=4)
            src = raw[w, g, HALF * h + lo].rearrange("p j (n i) -> p n j i", i=4)
            if eng == "v":
                nc.vector.tensor_copy(out=dst, in_=src)
            else:
                nc.scalar.copy(out=dst, in_=src)

        def quant_w(w, g, h):
            codes[w, g, h] = keep.tile([P, HALF], U32, name="codes_%s%d%d" % (w, g, h), align_bytes=64)
            scales[w, g, h] = keep.tile([P, HALF], U8, name="scales_%s%d%d" % (w, g, h), align_bytes=64)
            nc.vector.quantize_mx(out=codes[w, g, h][:].bitcast(FP8X4), scales=scales[w, g, h][:], in_=grouped[w, g, h][:].rearrange("p n j -> p (n j)"))

        def turn(kind, i):
            src = {"f": f_rows, "fm": fm, "out": res16}[kind][i][:].bitcast(F32)
            bank = psum.tile([P, 2, 2, P], F32, name="turned_%s%d" % (kind, i), tag="turned", bufs=4)
            turned[kind, i] = bank
            for g in range(2):
                for u in range(2):
                    if kind == "out":
                        cols = src[:, 256 * g + P * u : 256 * g + P * (u + 1)]
                    else:
                        cols = src[:, 256 * g + u : 256 * (g + 1) : 2]
                    nc.tensor.transpose(bank[:, g, u, :], cols, ident[:])

        def copy(eng, out, in_):
            if eng == "v":
                nc.vector.tensor_copy(out=out, in_=in_)
            else:
                nc.scalar.copy(out=out, in_=in_)

        def gather(eng, kind, i):
            grouped[kind, i] = work.tile([P, 2, P, 4], BF16, name="grouped_%s%d" % (kind, i), tag="grouped_" + kind, bufs=3, align_bytes=64)
            dst = grouped[kind, i][:].rearrange("p g m j -> p (g m j)").bitcast(F32).rearrange("p (g m u) -> p g m u", g=2, u=2)
            copy(eng, dst, turned[kind, i][:].rearrange("p g u m -> p g m u"))

        def gather_out(eng, i, g_lo, g_hi):
            lo, hi = group_of(WORD_GROUPS, i)
            if ("out", lo) not in grouped:
                grouped["out", lo] = keep.tile([P, 2, P * (hi - lo), 4], BF16, name="grouped_out%d" % lo, align_bytes=64)
            dst = grouped["out", lo][:, g_lo:g_hi, P * (i - lo) : P * (i - lo + 1), :].rearrange("p g m j -> p g (m j)").bitcast(F32)
            copy(eng, dst.rearrange("p g (m u) -> p g m u", u=2), turned["out", i, g_lo][:].rearrange("p g u m -> p g m u"))

        def turn_out(i, g_lo, g_hi):
            src = res16[i][:].bitcast(F32)
            bank = psum.tile([P, g_hi - g_lo, 2, P], F32, name="turned_out%d%d" % (i, g_lo), tag="turned", bufs=4)
            turned["out", i, g_lo] = bank
            for g in range(g_lo, g_hi):
                for u in range(2):
                    nc.tensor.transpose(bank[:, g - g_lo, u, :], src[:, 256 * g + P * u : 256 * g + P * (u + 1)], ident[:])

        def quant(kind, i):
            codes[kind, i] = work.tile([P, 2 * P], U32, name="codes_%s%d" % (kind, i), tag="codes_" + kind, bufs=4, align_bytes=64)
            scales[kind, i] = work.tile([P, 2 * P], U8, name="scales_%s%d" % (kind, i), tag="scales_" + kind, bufs=4, align_bytes=64)
            nc.vector.quantize_mx(out=codes[kind, i][:].bitcast(FP8X4), scales=scales[kind, i][:], in_=grouped[kind, i][:].rearrange("p g m j -> p (g m j)"))

        def multiply(kind, i, h):
            w = {"f": "r", "fm": "c"}[kind]
            acc[kind, i, h] = psum.tile([P, HALF], F32, name="acc_%s%d%d" % (kind, i, h), tag="acc_" + kind)
            for g in range(2):
                nc.tensor.matmul_mx(
                    out=acc[kind, i, h][:],
                    lhsT=codes[kind, i][:, P * g : P * (g + 1)].bitcast(FP8X4),
                    lhsT_scale=scales[kind, i][:, P * g : P * (g + 1)],
                    rhs=codes[w, g, h][:].bitcast(FP8X4),
                    rhs_scale=scales[w, g, h][:],
                    start=(g == 0),
                    stop=(g == 1),
                )

        def window(i):
            sig[i] = work.tile([P, N], F32, name="sig%d" % i, tag="sig", bufs=6)
            nc.scalar.activation(out=sig[i][:], in_=log_t[:], func=ACT.Sigmoid, scale=-1.0, bias=log_td[:, i : i + 1])

        def windowed(kind, i, h):
            cols = slice(HALF * h, HALF * (h + 1))
            if kind == "f":
                if h == 0:
                    fm[i] = work.tile([P, N], BF16, name="fm%d" % i, tag="fm")
                dst = fm[i]
            else:
                if h == 0:
                    res[i] = work.tile([P, N], F32, name="res%d" % i, tag="res", bufs=8)
                dst = res[i]
            nc.vector.scalar_tensor_tensor(out=dst[:, cols], in0=acc[kind, i, h][:], scalar=peak[:, i : i + 1], in1=sig[i][:, cols], op0=ALU.mult, op1=ALU.mult)

        def add_direct(eng, i, h):
            cols = slice(HALF * h, HALF * (h + 1))
            eng.tensor_tensor(out=res[i][:, cols], in0=res[i][:, cols], in1=fd_rows[i][:, cols], op=ALU.add)

        def store_res(i, lo, hi):
            nc.sync.dma_start(out=out_0[P * i : P * (i + 1), lo:hi], in_=res[i][:, lo:hi])

        def cast(eng, i, h):
            cols = slice(HALF * h, HALF * (h + 1))
            if h == 0:
                res16[i] = work.tile([P, N], BF16, name="res16_%d" % i, tag="res16", bufs=4)
            copy(
                eng,
                res16[i][:, cols].rearrange("p (u q e) -> p u q e", u=2, e=2),
                res[i][:, cols].rearrange("p (q u e) -> p u q e", u=2, e=2),
            )

        def group_of(groups, i):
            return [span for span in groups if span[0] <= i < span[1]][0]

        def quant_out(i, g):
            lo, hi = group_of(WORD_GROUPS, i)
            if (lo, hi) not in words:
                words[lo, hi] = keep.tile([P, 2, P * (hi - lo)], U32, name="words%d" % lo, align_bytes=64)
            s_lo, s_hi = group_of(SCALE_GROUPS, i)
            if (s_lo, s_hi) not in out_scales:
                out_scales[s_lo, s_hi] = keep.tile([P, 2, P * (s_hi - s_lo)], U8, name="out_scales%d" % s_lo, align_bytes=64)
            nc.vector.quantize_mx(
                out=words[lo, hi][:, g, :].bitcast(FP8X4),
                scales=out_scales[s_lo, s_hi][:, g, P * (lo - s_lo) : P * (hi - s_lo)],
                in_=grouped["out", lo][:, g, :, :].rearrange("p m j -> p (m j)"),
            )

        def store_words(k):
            lo, hi = WORD_GROUPS[k]
            dst = out_1.rearrange("g p m t -> p g (m t)").bitcast(I32)
            nc.sync.dma_start(out=dst[:, :, P * lo : P * hi], in_=words[lo, hi][:].bitcast(I32))

        def store_scales(k):
            s_lo, s_hi = SCALE_GROUPS[k]
            for q in range(4):
                queue = nc.scalar if (s_hi == TILES and q < 2) else nc.sync
                queue.dma_start(
                    out=out_2[:, 4 * q : 4 * q + 4, P * s_lo : P * s_hi].rearrange("g r m -> r g m").bitcast(I32),
                    in_=out_scales[s_lo, s_hi][32 * q : 32 * q + 4, :, :].bitcast(I32),
                )

        def add_rounded(i, h):
            cols = slice(HALF * h, HALF * (h + 1))
            nc.vector.tensor_tensor(
                out=res16[i][:, cols].rearrange("p (u q e) -> p u q e", u=2, e=2),
                in0=res[i][:, cols].rearrange("p (q u e) -> p u q e", u=2, e=2),
                in1=fd_rows[i][:, cols].rearrange("p (q u e) -> p u q e", u=2, e=2),
                op=ALU.add,
            )

        def turn_half(i, g):
            src = res16[i][:].bitcast(F32)
            turned["out", i, g] = psum.tile([P, 2, P], F32, name="turned_out%d%d" % (i, g), tag="turned", bufs=4)
            for u in range(2):
                nc.tensor.transpose(turned["out", i, g][:, u, :], src[:, 256 * g + P * u : 256 * g + P * (u + 1)], ident[:])

        def gather_half(eng, i, g):
            if g == 0:
                grouped["out", i] = work.tile([P, 2, P, 4], BF16, name="grouped_out%d" % i, tag="grouped_out", bufs=8, align_bytes=64)
            dst = grouped["out", i][:, g, :, :].rearrange("p m j -> p (m j)").bitcast(F32).rearrange("p (m u) -> p m u", u=2)
            copy(eng, dst, turned["out", i, g][:].rearrange("p u m -> p m u"))

        mag = keep.tile([P, P + 8], F32, name="mag")
        dec = keep.tile([P, P + 8], F32, name="dec")
        logc = keep.tile([P, P + 8], F32, name="logc")
        td32 = keep.tile([P, P], F32, name="td32")
        log_t = keep.tile([P, N], F32, name="log_t")
        log_td = keep.tile([P, TILES], F32, name="log_td")
        peak = keep.tile([P, TILES], F32, name="peak")
        spread = {}

        def spread_turn(h):
            spread[h] = psum.tile([P, 4, P], F32, name="spread%d" % h, tag="acc_fm")
            for j in range(4):
                nc.tensor.transpose(spread[h][:, j, :], logc[:, P + 4 * h + j : P + 4 * h + j + 1].to_broadcast([P, P]), ident[:])

        def spread_copy(eng, h):
            copy(eng, log_t[:, HALF * h : HALF * (h + 1)].rearrange("p (q j) -> p q j", j=4), spread[h][:].rearrange("p j q -> p q j"))

        nc.gpsimd.memset(times[:, 0 : 16 + P], 0.0)
        load_w("r", 0, 0, 256)
        interleave("v", "r", 0, 0, 0, 256)
        make_identity(nc, ident[:])
        nc.sync.dma_start(out=times[:, 16 + P :].rearrange("p (h j) -> p h j", h=2), in_=t.rearrange("(h p j) -> p h j", h=2, j=4))
        nc.sync.dma_start(out=times[0:TILES, 16 : 16 + P], in_=td.rearrange("(i q) -> i q", q=P))
        nc.vector.tensor_copy(out=td32[:], in_=times[:, 16 : 16 + P])
        load_w("r", 0, 256, 512)
        interleave("v", "r", 0, 0, 256, 512)
        quant_w("r", 0, 0)
        load_w("r", 1, 512, 1024)
        interleave("v", "r", 1, 1, 0, 256)
        interleave("v", "r", 1, 1, 256, 512)
        nc.scalar.activation(out=warm[:, 0:1], in_=times[:, 0:1], func=ACT.Exp)
        nc.scalar.activation(out=mag[:], in_=times[:, 16:], func=ACT.Abs, scale=4.0)
        nc.scalar.activation(out=dec[:], in_=mag[:], func=ACT.Exp, scale=-2.0)
        nc.scalar.activation(out=dec[:], in_=dec[:], func=ACT.Ln, bias=1.0)
        nc.vector.tensor_tensor(out=logc[:], in0=mag[:], in1=dec[:], op=ALU.add)
        small = psum.tile([P, 2, P], F32, name="small", tag="turned", bufs=4)
        nc.tensor.transpose(small[:, 0, :], logc[:, 0:P], ident[:])
        nc.tensor.transpose(small[:, 1, :], td32[:], ident[:])
        spread_turn(0)
        spread_turn(1)
        nc.scalar.activation(out=peak[:], in_=small[:, 1, 0:TILES], func=ACT.Sigmoid, scale=8.0)
        nc.scalar.copy(out=log_td[:], in_=small[:, 0, 0:TILES])
        spread_copy("s", 1)
        load_w("r", 0, 512, 1024)
        interleave("v", "r", 0, 1, 0, 256)
        interleave("v", "r", 0, 1, 256, 512)
        load_w("r", 1, 0, 512)
        interleave("v", "r", 1, 0, 0, 256)
        interleave("v", "r", 1, 0, 256, 512)
        quant_w("r", 1, 1)
        quant_w("r", 0, 1)
        quant_w("r", 1, 0)
        spread_copy("s", 0)
        window(0)
        load_w("c", 0, 0, 512)
        interleave("v", "c", 0, 0, 0, 256)
        interleave("v", "c", 0, 0, 256, 512)
        load_f(0)
        load_f(1)
        turn("f", 0)
        load_f(2)
        gather("s", "f", 0)
        turn("f", 1)
        load_f(3)
        quant("f", 0)
        gather("s", "f", 1)
        turn("f", 2)
        load_f(4)
        quant("f", 1)
        turn("f", 3)
        turn("f", 4)
        quant_w("c", 0, 0)
        gather("s", "f", 2)
        quant("f", 2)
        gather("s", "f", 3)
        quant("f", 3)
        multiply("f", 0, 0)
        windowed("f", 0, 0)
        multiply("f", 0, 1)
        windowed("f", 0, 1)
        window(1)
        gather("s", "f", 4)
        quant("f", 4)
        load_f(5)
        turn("f", 5)
        load_w("c", 0, 512, 1024)
        interleave("s", "c", 0, 1, 0, 256)
        interleave("v", "c", 0, 1, 256, 512)
        gather("s", "f", 5)
        multiply("f", 1, 0)
        windowed("f", 1, 0)
        multiply("f", 1, 1)
        windowed("f", 1, 1)
        load_w("c", 1, 0, 512)
        interleave("v", "c", 1, 0, 0, 256)
        interleave("s", "c", 1, 0, 256, 512)
        quant("f", 5)
        quant_w("c", 1, 0)
        turn("fm", 0)
        gather("s", "fm", 0)
        quant("fm", 0)
        window(2)
        load_f(6)
        turn("f", 6)
        gather("s", "f", 6)
        quant_w("c", 0, 1)
        load_fd(0)
        multiply("f", 2, 0)
        windowed("f", 2, 0)
        multiply("f", 2, 1)
        windowed("f", 2, 1)
        turn("fm", 1)
        quant("f", 6)
        gather("s", "fm", 1)
        quant("fm", 1)
        window(3)
        load_f(7)
        turn("f", 7)
        gather("s", "f", 7)
        load_fd(1)
        multiply("fm", 0, 0)
        windowed("fm", 0, 0)
        load_w("c", 1, 512, 1024)
        interleave("v", "c", 1, 1, 0, 256)
        multiply("f", 3, 0)
        windowed("f", 3, 0)
        multiply("f", 3, 1)
        windowed("f", 3, 1)
        turn("fm", 2)
        interleave("s", "c", 1, 1, 256, 512)
        quant_w("c", 1, 1)
        quant("f", 7)
        gather("s", "fm", 2)
        quant("fm", 2)
        load_fd(2)
        window(4)
        multiply("fm", 1, 0)
        windowed("fm", 1, 0)
        add_direct(nc.gpsimd, 0, 0)
        store_res(0, 0, 512)
        cast("s", 0, 0)
        multiply("f", 4, 0)
        windowed("f", 4, 0)
        multiply("f", 4, 1)
        windowed("f", 4, 1)
        turn("fm", 3)
        load_fd(3)
        multiply("fm", 0, 1)
        windowed("fm", 0, 1)
        gather("s", "fm", 3)
        quant("fm", 3)
        window(5)
        multiply("fm", 2, 0)
        windowed("fm", 2, 0)
        add_direct(nc.gpsimd, 1, 0)
        store_res(1, 0, 512)
        cast("s", 1, 0)
        multiply("f", 5, 0)
        windowed("f", 5, 0)
        multiply("f", 5, 1)
        windowed("f", 5, 1)
        turn("fm", 4)
        load_fd(4)
        multiply("fm", 1, 1)
        windowed("fm", 1, 1)
        add_direct(nc.gpsimd, 0, 1)
        store_res(0, 512, 1024)
        window(6)
        gather("s", "fm", 4)
        quant("fm", 4)
        multiply("fm", 3, 0)
        windowed("fm", 3, 0)
        add_direct(nc.gpsimd, 2, 0)
        store_res(2, 0, 512)
        multiply("f", 6, 0)
        windowed("f", 6, 0)
        multiply("f", 6, 1)
        windowed("f", 6, 1)
        turn("fm", 5)
        load_fd(5)
        multiply("fm", 2, 1)
        windowed("fm", 2, 1)
        add_direct(nc.gpsimd, 1, 1)
        store_res(1, 512, 1024)
        window(7)
        add_direct(nc.gpsimd, 3, 0)
        store_res(3, 0, 512)
        multiply("f", 7, 0)
        multiply("fm", 4, 0)
        windowed("f", 7, 0)
        multiply("f", 7, 1)
        windowed("fm", 4, 0)
        windowed("f", 7, 1)
        gather("s", "fm", 5)
        quant("fm", 5)
        load_fd(6)
        multiply("fm", 3, 1)
        windowed("fm", 3, 1)
        turn("fm", 6)
        add_direct(nc.gpsimd, 2, 1)
        store_res(2, 512, 1024)
        cast("s", 2, 0)
        cast("s", 0, 1)
        turn_out(0, 0, 2)
        add_direct(nc.vector, 4, 0)
        store_res(4, 0, 512)
        add_direct(nc.gpsimd, 3, 1)
        store_res(3, 512, 1024)
        load_fd(7)
        multiply("fm", 4, 1)
        windowed("fm", 4, 1)
        multiply("fm", 5, 0)
        windowed("fm", 5, 0)
        turn("fm", 7)
        gather("s", "fm", 6)
        quant("fm", 6)
        cast("s", 1, 1)
        turn_out(1, 0, 2)
        add_direct(nc.vector, 4, 1)
        store_res(4, 512, 1024)
        add_direct(nc.vector, 5, 0)
        store_res(5, 0, 512)
        multiply("fm", 5, 1)
        windowed("fm", 5, 1)
        cast("s", 2, 1)
        turn_out(2, 0, 2)
        multiply("fm", 6, 0)
        gather_out("s", 0, 0, 2)
        gather("s", "fm", 7)
        quant("fm", 7)
        windowed("fm", 6, 0)
        add_direct(nc.gpsimd, 5, 1)
        store_res(5, 512, 1024)
        multiply("fm", 6, 1)
        windowed("fm", 6, 1)
        add_direct(nc.vector, 6, 0)
        store_res(6, 0, 512)
        cast("s", 3, 0)
        cast("s", 3, 1)
        turn_out(3, 0, 2)
        add_direct(nc.gpsimd, 6, 1)
        store_res(6, 512, 1024)
        multiply("fm", 7, 0)
        multiply("fm", 7, 1)
        windowed("fm", 7, 0)
        windowed("fm", 7, 1)
        add_direct(nc.vector, 7, 0)
        store_res(7, 0, 512)
        add_direct(nc.vector, 7, 1)
        gather_out("s", 1, 0, 2)
        quant_out(1, 0)
        quant_out(1, 1)
        store_res(7, 512, 1024)
        store_words(0)
        cast("s", 4, 0)
        cast("s", 4, 1)
        gather_out("s", 2, 0, 2)
        turn_out(4, 0, 2)
        cast("s", 5, 0)
        cast("s", 5, 1)
        gather_out("s", 3, 0, 2)
        quant_out(3, 0)
        quant_out(3, 1)
        store_words(1)
        cast("s", 6, 0)
        cast("s", 6, 1)
        gather_out("s", 4, 0, 2)
        turn_out(5, 0, 2)
        turn_out(6, 0, 2)
        gather_out("s", 5, 0, 2)
        cast("s", 7, 0)
        cast("v", 7, 1)
        quant_out(5, 0)
        quant_out(5, 1)
        store_words(2)
        store_scales(0)
        gather_out("s", 6, 0, 2)
        quant_out(6, 0)
        quant_out(6, 1)
        store_words(3)
        turn_out(7, 0, 1)
        gather_out("v", 7, 0, 1)
        turn_out(7, 1, 2)
        quant_out(7, 0)
        gather_out("s", 7, 1, 2)
        quant_out(7, 1)
        store_words(4)
        store_scales(1)
